import numpy as np
import ml_dtypes


def mxq(x, axis, fmt="e4m3"):
    dtype, down = {"e4m3": (ml_dtypes.float8_e4m3fn, 7), "e5m2": (ml_dtypes.float8_e5m2, 14)}[fmt]
    v = np.moveaxis(np.asarray(x, np.float32).astype(ml_dtypes.bfloat16).astype(np.float64), axis, -1)
    blocks = v.reshape(v.shape[:-1] + (-1, 32))
    amax = np.abs(blocks).max(-1, keepdims=True)
    byte = np.maximum(np.where(amax > 0, np.frexp(amax)[1] - 1 + 127, 0) - down, 1)
    scale = np.exp2(byte - 127.0)
    codes = (blocks / scale).astype(np.float32).astype(dtype).astype(np.float64)
    return np.moveaxis((codes * scale).reshape(v.shape), -1, axis)


WIDE = False


def mx_kscale(k):
    if not WIDE:
        return np.ones(k)
    levels = np.array([10, -10, 5, -5, 0])
    if k % 512:
        return np.exp2(np.random.permutation(np.resize(levels, k // 32))).repeat(32)
    a = np.empty((k // 512, 16))
    for p in range(k // 512):
        a[p, :8] = np.random.permutation(np.resize(levels, 8))
        for g in range(8):
            far = levels[np.abs(levels - a[p, g]) >= 10]
            a[p, g + 8] = far[np.random.randint(len(far))]
    return np.exp2(a.ravel()).repeat(32)


def f64(x):
    return np.asarray(x).astype(np.float64)


E2M1 = np.array([0.0, 0.5, 1.0, 1.5, 2.0, 3.0, 4.0, 6.0, -0.0, -0.5, -1.0, -1.5, -2.0, -3.0, -4.0, -6.0])


def pack_weight(w, fmt):
    k, n = w.shape
    w = f64(np.asarray(w, np.float32).astype(ml_dtypes.bfloat16)).reshape(k // 32, 32, n)
    amax = np.abs(w).max(1)
    if fmt == "e4m3":
        byte = np.frexp(amax)[1] - 1 + 127 - 7
    else:
        mant, ex = np.frexp(amax / 6.0)
        byte = np.where(mant > 0.5, ex, ex - 1) + 127
    byte = np.clip(np.where(amax > 0, byte, 1), 1, 254)
    scaled = (w * np.exp2(127.0 - byte)[:, None, :]).reshape(k, n).astype(np.float32)
    by_word = np.ascontiguousarray(scaled.reshape(k // 512, 128, 4, n).transpose(0, 1, 3, 2))
    if fmt == "e4m3":
        words = by_word.astype(ml_dtypes.float8_e4m3fn).view(np.uint8)
    else:
        c = by_word.astype(ml_dtypes.float4_e2m1fn).view(np.uint8) & 0xF
        words = (c[..., 0::2] | (c[..., 1::2] << 4)).reshape(k // 512, 128, 2 * n)
    return np.ascontiguousarray(words), np.ascontiguousarray(byte.astype(np.uint8).reshape(k // 512, 16, n))


def unpack_weight(words, scales, fmt):
    g, _, n = scales.shape
    words = np.ascontiguousarray(words).reshape(g, 128, n, -1)
    if fmt == "e4m3":
        vals = words.view(ml_dtypes.float8_e4m3fn).astype(np.float64)
    else:
        nib = np.empty((g, 128, n, 4), np.uint8)
        nib[..., 0::2] = words & 0xF
        nib[..., 1::2] = words >> 4
        vals = E2M1[nib]
    vals = vals * np.repeat(np.exp2(scales.astype(np.float64) - 127.0), 8, axis=1)[..., None]
    return vals.transpose(0, 1, 3, 2).reshape(g * 512, n)


def softplus(v):
    return np.log(1.0 + np.exp(v))


K, L, Q, I = 512, 1024, 512, 1024


def setup_inputs():
    n = np.random.standard_normal
    fk = mx_kscale(K)
    fl = mx_kscale(L)
    qap = pack_weight(n((K, Q)) * 0.05 * fk[:, None], "e4m3")
    qbp = pack_weight(n((L, Q)) * 0.02 * fl[:, None], "e2m1")
    kbp = pack_weight(n((L, I)) / fl[:, None], "e4m3")
    return {
        "qa_words": qap[0],
        "qa_scales": qap[1],
        "ka": (n((K, I)) / fk[:, None]).astype(np.float32),
        "qb_words": qbp[0],
        "qb_scales": qbp[1],
        "kb_words": kbp[0],
        "kb_scales": kbp[1],
        "of": (np.random.uniform(0.0, 1.0, (1, I))).astype(np.float32),
    }


def reference(qa_words, qa_scales, ka, qb_words, qb_scales, kb_words, kb_scales, of):
    qau = unpack_weight(qa_words, qa_scales, "e4m3")
    qbu = unpack_weight(qb_words, qb_scales, "e2m1")
    kbu = unpack_weight(kb_words, kb_scales, "e4m3")
    kaq = mxq(f64(ka), 0, "e4m3")
    a = qau.T @ kaq + qbu.T @ kbu
    y = softplus(np.max(a, axis=1, keepdims=True) - a) - f64(of)
    return y

@@ -1,0 +1,245 @@
+from contextlib import ExitStack
+
+import concourse.mybir as mybir
+from concourse.masks import make_identity
+
+K, L, Q, I = 512, 1024, 512, 1024
+FLOPS = 2 * Q * I * (K + L)
+
+F32 = mybir.dt.float32
+BF16 = mybir.dt.bfloat16
+I32 = mybir.dt.int32
+U32 = mybir.dt.uint32
+U8 = mybir.dt.uint8
+FP8X4 = mybir.dt.float8_e4m3fn_x4
+FP4X4 = mybir.dt.float4_e2m1fn_x4
+ACT = mybir.ActivationFunctionType
+ALU = mybir.AluOpType
+AXIS = mybir.AxisListType
+
+P = 128
+PACK = 4
+BANK = 512
+QT = Q // P
+LP = L // (P * PACK)
+WIDTHS = (256, 256, 256, 128, 128)
+STARTS = tuple(sum(WIDTHS[:c]) for c in range(len(WIDTHS)))
+NC = len(WIDTHS)
+KB_LOADS = ((0, 256), (256, 768), (768, 1024))
+
+
+def tile_mix_behind_the_best_column_kernel(tc, qa_words, qa_scales, ka, qb_words, qb_scales, kb_words, kb_scales, of, out):
+    nc = tc.nc
+    with ExitStack() as ctx:
+        sb = ctx.enter_context(tc.tile_pool(name="sb", bufs=1))
+        psum = ctx.enter_context(tc.psum_pool(name="psum", bufs=1))
+        ctx.enter_context(tc.manual_schedule())
+
+        qa_c = sb.tile([P, Q], U32, name="qa_c", align_bytes=64)
+        qa_s = sb.tile([P, 1, Q], U8, name="qa_s", align_bytes=64)
+        qb_c = sb.tile([P, LP, 2 * Q], U8, name="qb_c", align_bytes=64)
+        qb_s = sb.tile([P, LP, Q], U8, name="qb_s", align_bytes=64)
+        kb_s = sb.tile([P, LP, I], U8, name="kb_s", align_bytes=64)
+        kb_c = [sb.tile([P, LP, hi - lo], U32, name="kb_c%d" % lo, align_bytes=64) for lo, hi in KB_LOADS]
+        ka_raw = [sb.tile([P, PACK, w], F32, name="ka_raw%d" % c) for c, w in enumerate(WIDTHS)]
+        ka_bf = [sb.tile([P, w, PACK], BF16, name="ka_bf%d" % c, align_bytes=64) for c, w in enumerate(WIDTHS)]
+        ka_c = [sb.tile([P, w], U32, name="ka_c%d" % c, align_bytes=64) for c, w in enumerate(WIDTHS)]
+        ka_s = [sb.tile([P, w], U8, name="ka_s%d" % c, align_bytes=64) for c, w in enumerate(WIDTHS)]
+        of_col = sb.tile([P, 2, PACK], F32, name="of_col")
+        of_row = sb.tile([P, I], F32, name="of_row")
+        ident = sb.tile([P, P], F32, name="ident")
+        neg_max = sb.tile([P, QT, NC], F32, name="neg_max")
+        neg_best = sb.tile([P, QT], F32, name="neg_best")
+        behind = sb.tile([P, QT, NC], F32, name="behind")
+        shrink = sb.tile([P, QT, NC], F32, name="shrink")
+        expo = sb.tile([P, QT, I], F32, name="expo")
+        shifted = sb.tile([P, QT, I], F32, name="shifted")
+        warm = sb.tile([P, 2], F32, name="warm")
+
+        def per_bank(c):
+            return BANK // WIDTHS[c]
+
+        nc.gpsimd.memset(qb_s[:].rearrange("p z n -> p (z n)").bitcast(I32), 0)
+        nc.vector.memset(kb_s[:].rearrange("p z n -> p (z n)").bitcast(I32), 0)
+        nc.vector.memset(qa_s[:].rearrange("p z n -> p (z n)").bitcast(I32), 0)
+        nc.vector.memset(warm[:, 0:1], 0.0)
+        make_identity(nc, ident[:])
+        nc.scalar.activation(out=warm[:, 1:2], in_=warm[:, 0:1], func=ACT.Exp)
+
+        def load_scales(plane, rows):
+            src = rows.rearrange("z r n -> r z n").bitcast(I32)
+            for g in range(4):
+                nc.sync.dma_start(out=plane[32 * g : 32 * g + 4, :].bitcast(I32), in_=src[4 * g : 4 * g + 4])
+
+        ka_v = ka.rearrange("(p j) n -> p j n", j=PACK)
+        kb_v = kb_words.rearrange("z p n t -> p z (n t)").bitcast(I32)
+
+        def load_ka(c):
+            nc.sync.dma_start(out=ka_raw[c][:], in_=ka_v[:, :, STARTS[c] : STARTS[c] + WIDTHS[c]])
+
+        def load_kb(n):
+            lo, hi = KB_LOADS[n]
+            nc.sync.dma_start(out=kb_c[n][:].bitcast(I32), in_=kb_v[:, :, lo:hi])
+
+        nc.sync.dma_start(out=of_col[:], in_=of[0].rearrange("(h p j) -> p h j", h=2, j=PACK))
+        load_scales(qb_s, qb_scales)
+        nc.sync.dma_start(out=qb_c[:].bitcast(I32), in_=qb_words.rearrange("z p b -> p z b").bitcast(I32))
+        load_kb(0)
+        load_scales(kb_s, kb_scales)
+        load_ka(0)
+        nc.sync.dma_start(out=qa_c[:].bitcast(I32), in_=qa_words[0].rearrange("p n t -> p (n t)").bitcast(I32))
+        load_scales(qa_s, qa_scales)
+        load_ka(1)
+        load_kb(1)
+        load_ka(2)
+        load_kb(2)
+        load_ka(3)
+        load_ka(4)
+
+        for h in range(2):
+            spread = psum.tile([P, PACK, P], F32, name="spread%d" % h, tag="bank%d" % (6 + h))
+            for j in range(PACK):
+                nc.tensor.transpose(spread[:, j, :], of_col[:, h, j : j + 1].to_broadcast([P, P]), ident[:])
+            nc.scalar.copy(
+                out=of_row[:, BANK * h : BANK * (h + 1)].rearrange("p (n j) -> p n j", j=PACK),
+                in_=spread[:].rearrange("p j n -> p n j"),
+            )
+
+        banks = {}
+        number = 0
+        for c in range(NC):
+            for b in range(QT // per_bank(c)):
+                banks[c, b] = psum.tile([P, per_bank(c), WIDTHS[c]], F32, name="acc%d" % number, tag="bank%d" % number)
+                number = number + 1
+
+        def cast(c, engine):
+            dst = ka_bf[c][:].rearrange("p (n i) t -> p n t i", i=4)
+            src = ka_raw[c][:].rearrange("p t (n i) -> p n t i", i=4)
+            if engine == "vector":
+                nc.vector.tensor_copy(out=dst, in_=src)
+            else:
+                nc.scalar.copy(out=dst, in_=src)
+
+        def quant(c):
+            nc.vector.quantize_mx(out=ka_c[c][:].bitcast(FP8X4), scales=ka_s[c][:], in_=ka_bf[c][:].rearrange("p n t -> p (n t)"))
+
+        def mm_kb(c, b):
+            n = [i for i, (lo, hi) in enumerate(KB_LOADS) if lo <= STARTS[c] < hi][0]
+            step = BANK if WIDTHS[c] == BANK else P
+            first = True
+            for u in range(per_bank(c)):
+                q = b * per_bank(c) + u
+                for z in range(LP):
+                    for o in range(0, WIDTHS[c], step):
+                        col = STARTS[c] + o
+                        loc = col - KB_LOADS[n][0]
+                        nc.tensor.matmul_mx(
+                            out=banks[c, b][:, u, o : o + step],
+                            lhsT=qb_c[:, z, 2 * P * q : 2 * P * (q + 1)].bitcast(FP4X4),
+                            lhsT_scale=qb_s[:, z, P * q : P * (q + 1)],
+                            rhs=kb_c[n][:, z, loc : loc + step].bitcast(FP8X4),
+                            rhs_scale=kb_s[:, z, col : col + step],
+                            start=first,
+                            stop=False,
+                        )
+                        first = False
+
+        def mm_ka(c, b):
+            for u in range(per_bank(c)):
+                q = b * per_bank(c) + u
+                nc.tensor.matmul_mx(
+                    out=banks[c, b][:, u, :],
+                    lhsT=qa_c[:, P * q : P * (q + 1)].bitcast(FP8X4),
+                    lhsT_scale=qa_s[:, 0, P * q : P * (q + 1)],
+                    rhs=ka_c[c][:].bitcast(FP8X4),
+                    rhs_scale=ka_s[c][:],
+                    start=False,
+                    stop=(u == per_bank(c) - 1),
+                )
+
+        def row_max(c, b):
+            n = per_bank(c)
+            nc.vector.tensor_reduce(out=neg_max[:, b * n : (b + 1) * n, c], in_=banks[c, b][:], axis=AXIS.X, op=ALU.max, negate=True)
+
+        def exps(c, b):
+            cols = slice(STARTS[c], STARTS[c] + WIDTHS[c])
+            for u in range(per_bank(c)):
+                q = b * per_bank(c) + u
+                nc.scalar.activation(out=expo[:, q, cols], in_=banks[c, b][:, u, :], func=ACT.Exp, bias=neg_max[:, q, c : c + 1])
+
+        def shift(c, b):
+            n = per_bank(c)
+            cols = slice(STARTS[c], STARTS[c] + WIDTHS[c])
+            nc.vector.tensor_tensor(
+                out=shifted[:, b * n : (b + 1) * n, cols],
+                in0=banks[c, b][:],
+                in1=of_row[:, cols].unsqueeze(1).to_broadcast([P, n, WIDTHS[c]]),
+                op=ALU.add,
+            )
+
+        cast(0, "vector")
+        quant(0)
+        cast(1, "scalar")
+        mm_kb(0, 0)
+        mm_kb(0, 1)
+        for b in range(2):
+            mm_ka(0, b)
+            row_max(0, b)
+            exps(0, b)
+        quant(1)
+        shift(0, 0)
+        shift(0, 1)
+        cast(2, "scalar")
+        mm_kb(1, 0)
+        mm_kb(1, 1)
+        for b in range(2):
+            mm_ka(1, b)
+            row_max(1, b)
+            exps(1, b)
+        quant(2)
+        cast(3, "vector")
+        cast(4, "vector")
+        quant(3)
+        quant(4)
+        mm_kb(2, 0)
+        mm_kb(2, 1)
+        for b in range(2):
+            mm_ka(2, b)
+            row_max(2, b)
+            exps(2, b)
+        mm_kb(3, 0)
+        mm_kb(4, 0)
+        for c in (3, 4):
+            mm_ka(c, 0)
+            row_max(c, 0)
+            exps(c, 0)
+        nc.vector.tensor_reduce(out=neg_best[:], in_=neg_max[:], axis=AXIS.X, op=ALU.min)
+        shift(1, 0)
+        nc.vector.tensor_tensor(out=behind[:], in0=neg_max[:], in1=neg_best[:].unsqueeze(2).to_broadcast([P, QT, NC]), op=ALU.subtract)
+        nc.scalar.activation(out=shrink[:], in_=behind[:], func=ACT.Exp, scale=-1.0)
+        shift(2, 0)
+        shift(3, 0)
+        shift(4, 0)
+
+        for q in range(QT):
+            if q == 2:
+                shift(1, 1)
+                shift(2, 1)
+            for h in range(2):
+                cols = slice(BANK * h, BANK * (h + 1))
+                soft = sb.tile([P, BANK], F32, name="soft%d_%d" % (q, h))
+                for c in range(NC):
+                    if STARTS[c] // BANK == h:
+                        lo = STARTS[c] - BANK * h
+                        nc.scalar.activation(
+                            out=soft[:, lo : lo + WIDTHS[c]],
+                            in_=expo[:, q, STARTS[c] : STARTS[c] + WIDTHS[c]],
+                            func=ACT.Ln,
+                            bias=1.0,
+                            scale=shrink[:, q, c : c + 1],
+                        )
+                res = sb.tile([P, BANK], F32, name="res%d_%d" % (q, h))
+                nc.vector.scalar_tensor_tensor(
+                    out=res[:], in0=soft[:], scalar=neg_best[:, q : q + 1], in1=shifted[:, q, cols], op0=ALU.subtract, op1=ALU.subtract
+                )
+                nc.sync.dma_start(out=out[P * q : P * (q + 1), cols], in_=res[:])

@@ -19,227 +19,205 @@ AXIS = mybir.AxisListType
 
 P = 128
 PACK = 4
-BANK = 512
-QT = Q // P
-LP = L // (P * PACK)
-WIDTHS = (256, 256, 256, 128, 128)
-STARTS = tuple(sum(WIDTHS[:c]) for c in range(len(WIDTHS)))
-NC = len(WIDTHS)
-KB_LOADS = ((0, 256), (256, 768), (768, 1024))
+ROW_TILES = Q // P
+L_PASSES = L // (P * PACK)
+CHUNK = 256
+CHUNKS = I // CHUNK
+PAIR = 2
+PAIRS = ROW_TILES // PAIR
+FP4_COLUMNS = 128
+VECTOR_SHARE_FIRST = 160
+VECTOR_SHARE = 96
 
 
-def tile_mix_behind_the_best_column_kernel(tc, qa_words, qa_scales, ka, qb_words, qb_scales, kb_words, kb_scales, of, out):
+def tile_mix_behind_the_best_column_kernel(
+    tc, qa_words, qa_scales, ka, qb_words, qb_scales, kb_words, kb_scales, of, out
+):
     nc = tc.nc
     with ExitStack() as ctx:
         sb = ctx.enter_context(tc.tile_pool(name="sb", bufs=1))
         psum = ctx.enter_context(tc.psum_pool(name="psum", bufs=1))
         ctx.enter_context(tc.manual_schedule())
 
-        qa_c = sb.tile([P, Q], U32, name="qa_c", align_bytes=64)
-        qa_s = sb.tile([P, 1, Q], U8, name="qa_s", align_bytes=64)
-        qb_c = sb.tile([P, LP, 2 * Q], U8, name="qb_c", align_bytes=64)
-        qb_s = sb.tile([P, LP, Q], U8, name="qb_s", align_bytes=64)
-        kb_s = sb.tile([P, LP, I], U8, name="kb_s", align_bytes=64)
-        kb_c = [sb.tile([P, LP, hi - lo], U32, name="kb_c%d" % lo, align_bytes=64) for lo, hi in KB_LOADS]
-        ka_raw = [sb.tile([P, PACK, w], F32, name="ka_raw%d" % c) for c, w in enumerate(WIDTHS)]
-        ka_bf = [sb.tile([P, w, PACK], BF16, name="ka_bf%d" % c, align_bytes=64) for c, w in enumerate(WIDTHS)]
-        ka_c = [sb.tile([P, w], U32, name="ka_c%d" % c, align_bytes=64) for c, w in enumerate(WIDTHS)]
-        ka_s = [sb.tile([P, w], U8, name="ka_s%d" % c, align_bytes=64) for c, w in enumerate(WIDTHS)]
-        of_col = sb.tile([P, 2, PACK], F32, name="of_col")
+        qa_codes = sb.tile([P, Q], U32, name="qa_codes", align_bytes=64)
+        qa_plane = sb.tile([P, 1, Q], U8, name="qa_plane", align_bytes=64)
+        qb_codes = sb.tile([P, L_PASSES, 2 * Q], U8, name="qb_codes", align_bytes=64)
+        qb_plane = sb.tile([P, L_PASSES, Q], U8, name="qb_plane", align_bytes=64)
+        kb_plane = sb.tile([P, L_PASSES, I], U8, name="kb_plane", align_bytes=64)
+        kb_codes = [sb.tile([P, L_PASSES, CHUNK], U32, name="kb_codes%d" % c, align_bytes=64) for c in range(CHUNKS)]
+        ka_raw = [sb.tile([P, PACK, CHUNK], F32, name="ka_raw%d" % c) for c in range(CHUNKS)]
+        ka_bf16 = [sb.tile([P, CHUNK, PACK], BF16, name="ka_bf16_%d" % c, align_bytes=64) for c in range(CHUNKS)]
+        ka_codes = [sb.tile([P, CHUNK], U32, name="ka_codes%d" % c, align_bytes=64) for c in range(CHUNKS)]
+        ka_plane = [sb.tile([P, CHUNK], U8, name="ka_plane%d" % c, align_bytes=64) for c in range(CHUNKS)]
+        of_column = sb.tile([P, I // P], F32, name="of_column")
         of_row = sb.tile([P, I], F32, name="of_row")
-        ident = sb.tile([P, P], F32, name="ident")
-        neg_max = sb.tile([P, QT, NC], F32, name="neg_max")
-        neg_best = sb.tile([P, QT], F32, name="neg_best")
-        behind = sb.tile([P, QT, NC], F32, name="behind")
-        shrink = sb.tile([P, QT, NC], F32, name="shrink")
-        expo = sb.tile([P, QT, I], F32, name="expo")
-        shifted = sb.tile([P, QT, I], F32, name="shifted")
-        warm = sb.tile([P, 2], F32, name="warm")
+        identity = sb.tile([P, P], F32, name="identity")
+        neg_chunk_max = sb.tile([P, ROW_TILES, CHUNKS], F32, name="neg_chunk_max")
+        neg_row_max = sb.tile([P, ROW_TILES], F32, name="neg_row_max")
+        rescale = sb.tile([P, ROW_TILES, CHUNKS], F32, name="rescale")
+        exps = sb.tile([P, ROW_TILES, I], F32, name="exps")
+        a_plus_of = sb.tile([P, ROW_TILES, I], F32, name="a_plus_of")
 
-        def per_bank(c):
-            return BANK // WIDTHS[c]
+        def columns(c):
+            return slice(c * CHUNK, (c + 1) * CHUNK)
 
-        nc.gpsimd.memset(qb_s[:].rearrange("p z n -> p (z n)").bitcast(I32), 0)
-        nc.vector.memset(kb_s[:].rearrange("p z n -> p (z n)").bitcast(I32), 0)
-        nc.vector.memset(qa_s[:].rearrange("p z n -> p (z n)").bitcast(I32), 0)
-        nc.vector.memset(warm[:, 0:1], 0.0)
-        make_identity(nc, ident[:])
-        nc.scalar.activation(out=warm[:, 1:2], in_=warm[:, 0:1], func=ACT.Exp)
+        nc.gpsimd.dma_start(out=of_column[:], in_=of[0].rearrange("(p j) -> p j", p=P))
+        for plane in (qb_plane, kb_plane, qa_plane):
+            nc.vector.memset(plane[:].rearrange("p z n -> p (z n)").bitcast(I32), 0)
+        make_identity(nc, identity[:])
 
-        def load_scales(plane, rows):
-            src = rows.rearrange("z r n -> r z n").bitcast(I32)
-            for g in range(4):
-                nc.sync.dma_start(out=plane[32 * g : 32 * g + 4, :].bitcast(I32), in_=src[4 * g : 4 * g + 4])
-
-        ka_v = ka.rearrange("(p j) n -> p j n", j=PACK)
-        kb_v = kb_words.rearrange("z p n t -> p z (n t)").bitcast(I32)
+        def load_scale_rows(plane, scales, rows):
+            by_row = scales.rearrange("z (g r) n -> r g z n", r=4)
+            for r in rows:
+                nc.sync.dma_start(out=plane[r:P:32].bitcast(I32), in_=by_row[r].bitcast(I32))
 
         def load_ka(c):
-            nc.sync.dma_start(out=ka_raw[c][:], in_=ka_v[:, :, STARTS[c] : STARTS[c] + WIDTHS[c]])
+            nc.sync.dma_start(out=ka_raw[c][:], in_=ka.rearrange("(p t) n -> p t n", t=PACK)[:, :, columns(c)])
 
-        def load_kb(n):
-            lo, hi = KB_LOADS[n]
-            nc.sync.dma_start(out=kb_c[n][:].bitcast(I32), in_=kb_v[:, :, lo:hi])
+        def load_kb(c):
+            words = kb_words.rearrange("z p n t -> p z (n t)").bitcast(I32)
+            nc.sync.dma_start(out=kb_codes[c][:].bitcast(I32), in_=words[:, :, columns(c)])
 
-        nc.sync.dma_start(out=of_col[:], in_=of[0].rearrange("(h p j) -> p h j", h=2, j=PACK))
-        load_scales(qb_s, qb_scales)
-        nc.sync.dma_start(out=qb_c[:].bitcast(I32), in_=qb_words.rearrange("z p b -> p z b").bitcast(I32))
+        nc.sync.dma_start(out=qb_codes[:].bitcast(I32), in_=qb_words.rearrange("z p b -> p z b").bitcast(I32))
+        load_scale_rows(qb_plane, qb_scales, range(4))
+        load_scale_rows(kb_plane, kb_scales, range(2))
         load_kb(0)
-        load_scales(kb_s, kb_scales)
+        load_scale_rows(kb_plane, kb_scales, range(2, 4))
         load_ka(0)
-        nc.sync.dma_start(out=qa_c[:].bitcast(I32), in_=qa_words[0].rearrange("p n t -> p (n t)").bitcast(I32))
-        load_scales(qa_s, qa_scales)
-        load_ka(1)
-        load_kb(1)
-        load_ka(2)
-        load_kb(2)
-        load_ka(3)
-        load_ka(4)
+        nc.sync.dma_start(out=qa_codes[:].bitcast(I32), in_=qa_words[0].rearrange("p n t -> p (n t)").bitcast(I32))
+        load_scale_rows(qa_plane, qa_scales, range(4))
+        for c in range(1, CHUNKS):
+            load_ka(c)
+            load_kb(c)
 
-        for h in range(2):
-            spread = psum.tile([P, PACK, P], F32, name="spread%d" % h, tag="bank%d" % (6 + h))
+        bank_tags = ["bank%d" % n for n in range(CHUNKS * PAIRS)]
+        for half in range(2):
+            spread = psum.tile([P, PACK, P], F32, name="spread%d" % half, tag=bank_tags[half - 2])
             for j in range(PACK):
-                nc.tensor.transpose(spread[:, j, :], of_col[:, h, j : j + 1].to_broadcast([P, P]), ident[:])
+                source = of_column[:, PACK * half + j : PACK * half + j + 1].to_broadcast([P, P])
+                nc.tensor.transpose(spread[:, j, :], source, identity[:])
             nc.scalar.copy(
-                out=of_row[:, BANK * h : BANK * (h + 1)].rearrange("p (n j) -> p n j", j=PACK),
+                out=of_row[:].rearrange("p (n j) -> p n j", n=P)[:, :, PACK * half : PACK * (half + 1)],
                 in_=spread[:].rearrange("p j n -> p n j"),
             )
 
-        banks = {}
-        number = 0
-        for c in range(NC):
-            for b in range(QT // per_bank(c)):
-                banks[c, b] = psum.tile([P, per_bank(c), WIDTHS[c]], F32, name="acc%d" % number, tag="bank%d" % number)
-                number = number + 1
+        sums = [
+            [psum.tile([P, PAIR, CHUNK], F32, name="sums%d_%d" % (c, b), tag=bank_tags[c * PAIRS + b]) for b in range(PAIRS)]
+            for c in range(CHUNKS)
+        ]
 
-        def cast(c, engine):
-            dst = ka_bf[c][:].rearrange("p (n i) t -> p n t i", i=4)
-            src = ka_raw[c][:].rearrange("p t (n i) -> p n t i", i=4)
-            if engine == "vector":
-                nc.vector.tensor_copy(out=dst, in_=src)
-            else:
-                nc.scalar.copy(out=dst, in_=src)
-
-        def quant(c):
-            nc.vector.quantize_mx(out=ka_c[c][:].bitcast(FP8X4), scales=ka_s[c][:], in_=ka_bf[c][:].rearrange("p n t -> p (n t)"))
-
-        def mm_kb(c, b):
-            n = [i for i, (lo, hi) in enumerate(KB_LOADS) if lo <= STARTS[c] < hi][0]
-            step = BANK if WIDTHS[c] == BANK else P
-            first = True
-            for u in range(per_bank(c)):
-                q = b * per_bank(c) + u
-                for z in range(LP):
-                    for o in range(0, WIDTHS[c], step):
-                        col = STARTS[c] + o
-                        loc = col - KB_LOADS[n][0]
-                        nc.tensor.matmul_mx(
-                            out=banks[c, b][:, u, o : o + step],
-                            lhsT=qb_c[:, z, 2 * P * q : 2 * P * (q + 1)].bitcast(FP4X4),
-                            lhsT_scale=qb_s[:, z, P * q : P * (q + 1)],
-                            rhs=kb_c[n][:, z, loc : loc + step].bitcast(FP8X4),
-                            rhs_scale=kb_s[:, z, col : col + step],
-                            start=first,
-                            stop=False,
-                        )
-                        first = False
-
-        def mm_ka(c, b):
-            for u in range(per_bank(c)):
-                q = b * per_bank(c) + u
-                nc.tensor.matmul_mx(
-                    out=banks[c, b][:, u, :],
-                    lhsT=qa_c[:, P * q : P * (q + 1)].bitcast(FP8X4),
-                    lhsT_scale=qa_s[:, 0, P * q : P * (q + 1)],
-                    rhs=ka_c[c][:].bitcast(FP8X4),
-                    rhs_scale=ka_s[c][:],
-                    start=False,
-                    stop=(u == per_bank(c) - 1),
+        def round_and_interleave(c, split):
+            def views(cols):
+                return (
+                    ka_bf16[c][:, cols, :].rearrange("p (n i) t -> p n t i", i=4),
+                    ka_raw[c][:, :, cols].rearrange("p t (n i) -> p n t i", i=4),
                 )
 
-        def row_max(c, b):
-            n = per_bank(c)
-            nc.vector.tensor_reduce(out=neg_max[:, b * n : (b + 1) * n, c], in_=banks[c, b][:], axis=AXIS.X, op=ALU.max, negate=True)
+            target, source = views(slice(split, CHUNK))
+            nc.scalar.copy(out=target, in_=source)
+            target, source = views(slice(0, split))
+            nc.vector.tensor_copy(out=target, in_=source)
 
-        def exps(c, b):
-            cols = slice(STARTS[c], STARTS[c] + WIDTHS[c])
-            for u in range(per_bank(c)):
-                q = b * per_bank(c) + u
-                nc.scalar.activation(out=expo[:, q, cols], in_=banks[c, b][:, u, :], func=ACT.Exp, bias=neg_max[:, q, c : c + 1])
+        def quantise(c):
+            nc.vector.quantize_mx(
+                out=ka_codes[c][:].bitcast(FP8X4),
+                scales=ka_plane[c][:],
+                in_=ka_bf16[c][:].rearrange("p n t -> p (n t)"),
+            )
 
-        def shift(c, b):
-            n = per_bank(c)
-            cols = slice(STARTS[c], STARTS[c] + WIDTHS[c])
+        def multiply(c):
+            for b in range(PAIRS):
+                for u in range(PAIR):
+                    q = b * PAIR + u
+                    for z in range(L_PASSES):
+                        for at in range(0, CHUNK, FP4_COLUMNS):
+                            nc.tensor.matmul_mx(
+                                out=sums[c][b][:, u, at : at + FP4_COLUMNS],
+                                lhsT=qb_codes[:, z, 2 * P * q : 2 * P * (q + 1)].bitcast(FP4X4),
+                                lhsT_scale=qb_plane[:, z, P * q : P * (q + 1)],
+                                rhs=kb_codes[c][:, z, at : at + FP4_COLUMNS].bitcast(FP8X4),
+                                rhs_scale=kb_plane[:, z, c * CHUNK + at : c * CHUNK + at + FP4_COLUMNS],
+                                start=(u == 0 and z == 0 and at == 0),
+                                stop=False,
+                            )
+            for b in range(PAIRS):
+                for u in range(PAIR):
+                    q = b * PAIR + u
+                    nc.tensor.matmul_mx(
+                        out=sums[c][b][:, u, :],
+                        lhsT=qa_codes[:, P * q : P * (q + 1)].bitcast(FP8X4),
+                        lhsT_scale=qa_plane[:, 0, P * q : P * (q + 1)],
+                        rhs=ka_codes[c][:].bitcast(FP8X4),
+                        rhs_scale=ka_plane[c][:],
+                        start=False,
+                        stop=(u == PAIR - 1),
+                    )
+
+        def chunk_max(c, b):
+            nc.vector.tensor_reduce(
+                out=neg_chunk_max[:, b * PAIR : (b + 1) * PAIR, c], in_=sums[c][b][:], axis=AXIS.X, op=ALU.max, negate=True
+            )
+
+        def exponentials(c, b):
+            for u in range(PAIR):
+                q = b * PAIR + u
+                nc.scalar.activation(
+                    out=exps[:, q, columns(c)], in_=sums[c][b][:, u, :], func=ACT.Exp, bias=neg_chunk_max[:, q, c : c + 1]
+                )
+
+        def add_offset(c, b):
             nc.vector.tensor_tensor(
-                out=shifted[:, b * n : (b + 1) * n, cols],
-                in0=banks[c, b][:],
-                in1=of_row[:, cols].unsqueeze(1).to_broadcast([P, n, WIDTHS[c]]),
+                out=a_plus_of[:, b * PAIR : (b + 1) * PAIR, columns(c)],
+                in0=sums[c][b][:],
+                in1=of_row[:, columns(c)].unsqueeze(1).to_broadcast([P, PAIR, CHUNK]),
                 op=ALU.add,
             )
 
-        cast(0, "vector")
-        quant(0)
-        cast(1, "scalar")
-        mm_kb(0, 0)
-        mm_kb(0, 1)
-        for b in range(2):
-            mm_ka(0, b)
-            row_max(0, b)
-            exps(0, b)
-        quant(1)
-        shift(0, 0)
-        shift(0, 1)
-        cast(2, "scalar")
-        mm_kb(1, 0)
-        mm_kb(1, 1)
-        for b in range(2):
-            mm_ka(1, b)
-            row_max(1, b)
-            exps(1, b)
-        quant(2)
-        cast(3, "vector")
-        cast(4, "vector")
-        quant(3)
-        quant(4)
-        mm_kb(2, 0)
-        mm_kb(2, 1)
-        for b in range(2):
-            mm_ka(2, b)
-            row_max(2, b)
-            exps(2, b)
-        mm_kb(3, 0)
-        mm_kb(4, 0)
-        for c in (3, 4):
-            mm_ka(c, 0)
-            row_max(c, 0)
-            exps(c, 0)
-        nc.vector.tensor_reduce(out=neg_best[:], in_=neg_max[:], axis=AXIS.X, op=ALU.min)
-        shift(1, 0)
-        nc.vector.tensor_tensor(out=behind[:], in0=neg_max[:], in1=neg_best[:].unsqueeze(2).to_broadcast([P, QT, NC]), op=ALU.subtract)
-        nc.scalar.activation(out=shrink[:], in_=behind[:], func=ACT.Exp, scale=-1.0)
-        shift(2, 0)
-        shift(3, 0)
-        shift(4, 0)
+        round_and_interleave(0, VECTOR_SHARE_FIRST)
+        quantise(0)
+        multiply(0)
+        last = CHUNKS - 1
+        for c in range(1, CHUNKS):
+            round_and_interleave(c, VECTOR_SHARE)
+            if c > 1:
+                exponentials(c - 2, 1)
+            chunk_max(c - 1, 0)
+            exponentials(c - 1, 0)
+            quantise(c)
+            chunk_max(c - 1, 1)
+            if c < last:
+                add_offset(c - 1, 0)
+            multiply(c)
+        exponentials(last - 1, 1)
+        for b in range(PAIRS):
+            chunk_max(last, b)
+            exponentials(last, b)
+        add_offset(last - 1, 0)
+        nc.vector.tensor_reduce(out=neg_row_max[:], in_=neg_chunk_max[:], axis=AXIS.X, op=ALU.min)
+        for q in range(ROW_TILES):
+            nc.scalar.activation(
+                out=rescale[:, q, :], in_=neg_chunk_max[:, q, :], func=ACT.Exp, scale=-1.0, bias=neg_row_max[:, q : q + 1]
+            )
+        add_offset(last, 0)
+        for c in range(CHUNKS):
+            add_offset(c, 1)
 
-        for q in range(QT):
-            if q == 2:
-                shift(1, 1)
-                shift(2, 1)
-            for h in range(2):
-                cols = slice(BANK * h, BANK * (h + 1))
-                soft = sb.tile([P, BANK], F32, name="soft%d_%d" % (q, h))
-                for c in range(NC):
-                    if STARTS[c] // BANK == h:
-                        lo = STARTS[c] - BANK * h
-                        nc.scalar.activation(
-                            out=soft[:, lo : lo + WIDTHS[c]],
-                            in_=expo[:, q, STARTS[c] : STARTS[c] + WIDTHS[c]],
-                            func=ACT.Ln,
-                            bias=1.0,
-                            scale=shrink[:, q, c : c + 1],
-                        )
-                res = sb.tile([P, BANK], F32, name="res%d_%d" % (q, h))
+        for q in range(ROW_TILES):
+            pieces = ((0, 1), (2, 3)) if q < ROW_TILES - 1 else ((0, 1), (2,), (3,))
+            for piece in pieces:
+                cols = slice(piece[0] * CHUNK, (piece[-1] + 1) * CHUNK)
+                logs = sb.tile([P, len(piece), CHUNK], F32, name="logs%d_%d" % (q, piece[0]))
+                for n, c in enumerate(piece):
+                    nc.scalar.activation(
+                        out=logs[:, n, :], in_=exps[:, q, columns(c)], func=ACT.Ln, bias=1.0, scale=rescale[:, q, c : c + 1]
+                    )
+                result = sb.tile([P, len(piece) * CHUNK], F32, name="result%d_%d" % (q, piece[0]))
                 nc.vector.scalar_tensor_tensor(
-                    out=res[:], in0=soft[:], scalar=neg_best[:, q : q + 1], in1=shifted[:, q, cols], op0=ALU.subtract, op1=ALU.subtract
+                    out=result[:],
+                    in0=logs[:].rearrange("p n w -> p (n w)"),
+                    scalar=neg_row_max[:, q : q + 1],
+                    in1=a_plus_of[:, q, cols],
+                    op0=ALU.subtract,
+                    op1=ALU.subtract,
                 )
-                nc.sync.dma_start(out=out[P * q : P * (q + 1), cols], in_=res[:])
+                nc.sync.dma_start(out=out[P * q : P * (q + 1), cols], in_=result[:])

@@ -57,11 +57,11 @@ def tile_mix_behind_the_best_column_kernel(
         rescale = sb.tile([P, ROW_TILES, CHUNKS], F32, name="rescale")
         exps = sb.tile([P, ROW_TILES, I], F32, name="exps")
         a_plus_of = sb.tile([P, ROW_TILES, I], F32, name="a_plus_of")
+        neg_a = sb.tile([P, PAIR, CHUNK], F32, name="neg_a")
 
         def columns(c):
             return slice(c * CHUNK, (c + 1) * CHUNK)
 
-        nc.gpsimd.dma_start(out=of_column[:], in_=of[0].rearrange("(p j) -> p j", p=P))
         for plane in (qb_plane, kb_plane, qa_plane):
             nc.vector.memset(plane[:].rearrange("p z n -> p (z n)").bitcast(I32), 0)
         make_identity(nc, identity[:])
@@ -78,6 +78,7 @@ def tile_mix_behind_the_best_column_kernel(
             words = kb_words.rearrange("z p n t -> p z (n t)").bitcast(I32)
             nc.sync.dma_start(out=kb_codes[c][:].bitcast(I32), in_=words[:, :, columns(c)])
 
+        nc.sync.dma_start(out=of_column[:], in_=of[0].rearrange("(p j) -> p j", p=P))
         nc.sync.dma_start(out=qb_codes[:].bitcast(I32), in_=qb_words.rearrange("z p b -> p z b").bitcast(I32))
         load_scale_rows(qb_plane, qb_scales, range(4))
         load_scale_rows(kb_plane, kb_scales, range(2))
@@ -125,33 +126,58 @@ def tile_mix_behind_the_best_column_kernel(
                 in_=ka_bf16[c][:].rearrange("p n t -> p (n t)"),
             )
 
+        def multiply_b(c, b):
+            for u in range(PAIR):
+                q = b * PAIR + u
+                for z in range(L_PASSES):
+                    for at in range(0, CHUNK, FP4_COLUMNS):
+                        nc.tensor.matmul_mx(
+                            out=sums[c][b][:, u, at : at + FP4_COLUMNS],
+                            lhsT=qb_codes[:, z, 2 * P * q : 2 * P * (q + 1)].bitcast(FP4X4),
+                            lhsT_scale=qb_plane[:, z, P * q : P * (q + 1)],
+                            rhs=kb_codes[c][:, z, at : at + FP4_COLUMNS].bitcast(FP8X4),
+                            rhs_scale=kb_plane[:, z, c * CHUNK + at : c * CHUNK + at + FP4_COLUMNS],
+                            start=(u == 0 and z == 0 and at == 0),
+                            stop=False,
+                        )
+
+        def multiply_a(c, b):
+            for u in range(PAIR):
+                q = b * PAIR + u
+                nc.tensor.matmul_mx(
+                    out=sums[c][b][:, u, :],
+                    lhsT=qa_codes[:, P * q : P * (q + 1)].bitcast(FP8X4),
+                    lhsT_scale=qa_plane[:, 0, P * q : P * (q + 1)],
+                    rhs=ka_codes[c][:].bitcast(FP8X4),
+                    rhs_scale=ka_plane[c][:],
+                    start=False,
+                    stop=(u == PAIR - 1),
+                )
+
         def multiply(c):
             for b in range(PAIRS):
-                for u in range(PAIR):
-                    q = b * PAIR + u
-                    for z in range(L_PASSES):
-                        for at in range(0, CHUNK, FP4_COLUMNS):
-                            nc.tensor.matmul_mx(
-                                out=sums[c][b][:, u, at : at + FP4_COLUMNS],
-                                lhsT=qb_codes[:, z, 2 * P * q : 2 * P * (q + 1)].bitcast(FP4X4),
-                                lhsT_scale=qb_plane[:, z, P * q : P * (q + 1)],
-                                rhs=kb_codes[c][:, z, at : at + FP4_COLUMNS].bitcast(FP8X4),
-                                rhs_scale=kb_plane[:, z, c * CHUNK + at : c * CHUNK + at + FP4_COLUMNS],
-                                start=(u == 0 and z == 0 and at == 0),
-                                stop=False,
-                            )
+                multiply_b(c, b)
             for b in range(PAIRS):
-                for u in range(PAIR):
-                    q = b * PAIR + u
-                    nc.tensor.matmul_mx(
-                        out=sums[c][b][:, u, :],
-                        lhsT=qa_codes[:, P * q : P * (q + 1)].bitcast(FP8X4),
-                        lhsT_scale=qa_plane[:, 0, P * q : P * (q + 1)],
-                        rhs=ka_codes[c][:].bitcast(FP8X4),
-                        rhs_scale=ka_plane[c][:],
-                        start=False,
-                        stop=(u == PAIR - 1),
-                    )
+                multiply_a(c, b)
+
+        def chunk_max_with_copy(c, b):
+            for u in range(PAIR):
+                q = b * PAIR + u
+                nc.vector.tensor_scalar(
+                    out=neg_a[:, u, :],
+                    in0=sums[c][b][:, u, :],
+                    scalar1=-1.0,
+                    scalar2=None,
+                    op0=ALU.mult,
+                    op1=ALU.min,
+                    accum_out=neg_chunk_max[:, q, c : c + 1],
+                )
+                nc.gpsimd.tensor_tensor(
+                    out=a_plus_of[:, q, columns(c)], in0=of_row[:, columns(c)], in1=neg_a[:, u, :], op=ALU.subtract
+                )
+                nc.scalar.activation(
+                    out=exps[:, q, columns(c)], in_=neg_a[:, u, :], func=ACT.Exp, scale=-1.0, bias=neg_chunk_max[:, q, c : c + 1]
+                )
 
         def chunk_max(c, b):
             nc.vector.tensor_reduce(
@@ -177,7 +203,7 @@ def tile_mix_behind_the_best_column_kernel(
         quantise(0)
         multiply(0)
         last = CHUNKS - 1
-        for c in range(1, CHUNKS):
+        for c in range(1, last):
             round_and_interleave(c, VECTOR_SHARE)
             if c > 1:
                 exponentials(c - 2, 1)
@@ -185,25 +211,33 @@ def tile_mix_behind_the_best_column_kernel(
             exponentials(c - 1, 0)
             quantise(c)
             chunk_max(c - 1, 1)
-            if c < last:
-                add_offset(c - 1, 0)
+            if c == 1:
+                add_offset(0, 0)
             multiply(c)
-        exponentials(last - 1, 1)
+        round_and_interleave(last, VECTOR_SHARE_FIRST)
+        exponentials(last - 2, 1)
+        quantise(last)
+        chunk_max(last - 1, 0)
+        exponentials(last - 1, 0)
+        chunk_max_with_copy(last - 1, 1)
         for b in range(PAIRS):
+            multiply_b(last, b)
+            multiply_a(last, b)
             chunk_max(last, b)
             exponentials(last, b)
-        add_offset(last - 1, 0)
+        add_offset(1, 0)
         nc.vector.tensor_reduce(out=neg_row_max[:], in_=neg_chunk_max[:], axis=AXIS.X, op=ALU.min)
         for q in range(ROW_TILES):
             nc.scalar.activation(
                 out=rescale[:, q, :], in_=neg_chunk_max[:, q, :], func=ACT.Exp, scale=-1.0, bias=neg_row_max[:, q : q + 1]
             )
-        add_offset(last, 0)
-        for c in range(CHUNKS):
+        for c in range(2, CHUNKS):
+            add_offset(c, 0)
+        for c in (0, 1, last):
             add_offset(c, 1)
 
         for q in range(ROW_TILES):
-            pieces = ((0, 1), (2, 3)) if q < ROW_TILES - 1 else ((0, 1), (2,), (3,))
+            pieces = ((0, 1), (2, 3))
             for piece in pieces:
                 cols = slice(piece[0] * CHUNK, (piece[-1] + 1) * CHUNK)
                 logs = sb.tile([P, len(piece), CHUNK], F32, name="logs%d_%d" % (q, piece[0]))

@@ -21,13 +21,11 @@ P = 128
 PACK = 4
 ROW_TILES = Q // P
 L_PASSES = L // (P * PACK)
-CHUNK = 256
-CHUNKS = I // CHUNK
-PAIR = 2
-PAIRS = ROW_TILES // PAIR
-FP4_COLUMNS = 128
-VECTOR_SHARE_FIRST = 160
-VECTOR_SHARE = 96
+BANK = 512
+STRIP = 256
+CHUNKS = ((0, 512), (512, 768), (768, 1024))
+VECTOR_SHARE = 160
+GPSIMD_SHARE = 128
 
 
 def tile_mix_behind_the_best_column_kernel(
@@ -39,28 +37,33 @@ def tile_mix_behind_the_best_column_kernel(
         psum = ctx.enter_context(tc.psum_pool(name="psum", bufs=1))
         ctx.enter_context(tc.manual_schedule())
 
+        widths = [hi - lo for lo, hi in CHUNKS]
+        strips = range(I // STRIP)
         qa_codes = sb.tile([P, Q], U32, name="qa_codes", align_bytes=64)
         qa_plane = sb.tile([P, 1, Q], U8, name="qa_plane", align_bytes=64)
         qb_codes = sb.tile([P, L_PASSES, 2 * Q], U8, name="qb_codes", align_bytes=64)
         qb_plane = sb.tile([P, L_PASSES, Q], U8, name="qb_plane", align_bytes=64)
         kb_plane = sb.tile([P, L_PASSES, I], U8, name="kb_plane", align_bytes=64)
-        kb_codes = [sb.tile([P, L_PASSES, CHUNK], U32, name="kb_codes%d" % c, align_bytes=64) for c in range(CHUNKS)]
-        ka_raw = [sb.tile([P, PACK, CHUNK], F32, name="ka_raw%d" % c) for c in range(CHUNKS)]
-        ka_bf16 = [sb.tile([P, CHUNK, PACK], BF16, name="ka_bf16_%d" % c, align_bytes=64) for c in range(CHUNKS)]
-        ka_codes = [sb.tile([P, CHUNK], U32, name="ka_codes%d" % c, align_bytes=64) for c in range(CHUNKS)]
-        ka_plane = [sb.tile([P, CHUNK], U8, name="ka_plane%d" % c, align_bytes=64) for c in range(CHUNKS)]
+        kb_codes = [sb.tile([P, L_PASSES, w], U32, name="kb_codes%d" % c, align_bytes=64) for c, w in enumerate(widths)]
+        ka_raw = [sb.tile([P, PACK, w], F32, name="ka_raw%d" % c) for c, w in enumerate(widths)]
+        ka_bf16 = [sb.tile([P, STRIP, PACK], BF16, name="ka_bf16_%d" % s, align_bytes=64) for s in strips]
+        ka_codes = [sb.tile([P, STRIP], U32, name="ka_codes%d" % s, align_bytes=64) for s in strips]
+        ka_plane = [sb.tile([P, STRIP], U8, name="ka_plane%d" % s, align_bytes=64) for s in strips]
         of_column = sb.tile([P, I // P], F32, name="of_column")
         of_row = sb.tile([P, I], F32, name="of_row")
         identity = sb.tile([P, P], F32, name="identity")
-        neg_chunk_max = sb.tile([P, ROW_TILES, CHUNKS], F32, name="neg_chunk_max")
+        neg_chunk_max = sb.tile([P, ROW_TILES, len(CHUNKS)], F32, name="neg_chunk_max")
         neg_row_max = sb.tile([P, ROW_TILES], F32, name="neg_row_max")
-        rescale = sb.tile([P, ROW_TILES, CHUNKS], F32, name="rescale")
+        rescale = sb.tile([P, ROW_TILES, len(CHUNKS)], F32, name="rescale")
         exps = sb.tile([P, ROW_TILES, I], F32, name="exps")
         a_plus_of = sb.tile([P, ROW_TILES, I], F32, name="a_plus_of")
-        neg_a = sb.tile([P, PAIR, CHUNK], F32, name="neg_a")
 
         def columns(c):
-            return slice(c * CHUNK, (c + 1) * CHUNK)
+            return slice(CHUNKS[c][0], CHUNKS[c][1])
+
+        def rows_of_bank(c, b):
+            count = BANK // widths[c]
+            return range(b * count, (b + 1) * count)
 
         for plane in (qb_plane, kb_plane, qa_plane):
             nc.vector.memset(plane[:].rearrange("p z n -> p (z n)").bitcast(I32), 0)
@@ -87,11 +90,11 @@ def tile_mix_behind_the_best_column_kernel(
         load_ka(0)
         nc.sync.dma_start(out=qa_codes[:].bitcast(I32), in_=qa_words[0].rearrange("p n t -> p (n t)").bitcast(I32))
         load_scale_rows(qa_plane, qa_scales, range(4))
-        for c in range(1, CHUNKS):
+        for c in range(1, len(CHUNKS)):
             load_ka(c)
             load_kb(c)
 
-        bank_tags = ["bank%d" % n for n in range(CHUNKS * PAIRS)]
+        bank_tags = ["bank%d" % n for n in range(8)]
         for half in range(2):
             spread = psum.tile([P, PACK, P], F32, name="spread%d" % half, tag=bank_tags[half - 2])
             for j in range(PACK):
@@ -102,67 +105,101 @@ def tile_mix_behind_the_best_column_kernel(
                 in_=spread[:].rearrange("p j n -> p n j"),
             )
 
-        sums = [
-            [psum.tile([P, PAIR, CHUNK], F32, name="sums%d_%d" % (c, b), tag=bank_tags[c * PAIRS + b]) for b in range(PAIRS)]
-            for c in range(CHUNKS)
-        ]
+        sums = []
+        for c, w in enumerate(widths):
+            first = ROW_TILES * CHUNKS[c][0] // BANK
+            sums.append(
+                [
+                    psum.tile([P, BANK // w, w], F32, name="sums%d_%d" % (c, b), tag=bank_tags[first + b])
+                    for b in range(ROW_TILES * w // BANK)
+                ]
+            )
 
-        def round_and_interleave(c, split):
-            def views(cols):
-                return (
-                    ka_bf16[c][:, cols, :].rearrange("p (n i) t -> p n t i", i=4),
-                    ka_raw[c][:, :, cols].rearrange("p t (n i) -> p n t i", i=4),
-                )
+        def strip_views(c, s, lo, hi):
+            at = s * STRIP - CHUNKS[c][0]
+            return ka_bf16[s][:, lo:hi, :], ka_raw[c][:, :, at + lo : at + hi]
 
-            target, source = views(slice(split, CHUNK))
-            nc.scalar.copy(out=target, in_=source)
-            target, source = views(slice(0, split))
-            nc.vector.tensor_copy(out=target, in_=source)
+        def round_on_scalar(c, s, lo):
+            target, source = strip_views(c, s, lo, STRIP)
+            nc.scalar.copy(out=target.rearrange("p (n i) t -> p n t i", i=4), in_=source.rearrange("p t (n i) -> p n t i", i=4))
 
-        def quantise(c):
+        def round_on_vector(c, s, hi):
+            target, source = strip_views(c, s, 0, hi)
+            nc.vector.tensor_copy(out=target.rearrange("p (n i) t -> p n t i", i=4), in_=source.rearrange("p t (n i) -> p n t i", i=4))
+
+        def round_on_gpsimd(c, s, hi):
+            target, source = strip_views(c, s, 0, hi)
+            nc.gpsimd.tensor_scalar(
+                out=target, in0=source.rearrange("p t n -> p n t"), scalar1=1.0, scalar2=0.0, op0=ALU.mult, op1=ALU.add
+            )
+
+        def quantise(s):
             nc.vector.quantize_mx(
-                out=ka_codes[c][:].bitcast(FP8X4),
-                scales=ka_plane[c][:],
-                in_=ka_bf16[c][:].rearrange("p n t -> p (n t)"),
+                out=ka_codes[s][:].bitcast(FP8X4),
+                scales=ka_plane[s][:],
+                in_=ka_bf16[s][:].rearrange("p n t -> p (n t)"),
             )
 
         def multiply_b(c, b):
-            for u in range(PAIR):
-                q = b * PAIR + u
+            step = BANK if widths[c] == BANK else P
+            for u, q in enumerate(rows_of_bank(c, b)):
                 for z in range(L_PASSES):
-                    for at in range(0, CHUNK, FP4_COLUMNS):
+                    for at in range(0, widths[c], step):
                         nc.tensor.matmul_mx(
-                            out=sums[c][b][:, u, at : at + FP4_COLUMNS],
+                            out=sums[c][b][:, u, at : at + step],
                             lhsT=qb_codes[:, z, 2 * P * q : 2 * P * (q + 1)].bitcast(FP4X4),
                             lhsT_scale=qb_plane[:, z, P * q : P * (q + 1)],
-                            rhs=kb_codes[c][:, z, at : at + FP4_COLUMNS].bitcast(FP8X4),
-                            rhs_scale=kb_plane[:, z, c * CHUNK + at : c * CHUNK + at + FP4_COLUMNS],
+                            rhs=kb_codes[c][:, z, at : at + step].bitcast(FP8X4),
+                            rhs_scale=kb_plane[:, z, CHUNKS[c][0] + at : CHUNKS[c][0] + at + step],
                             start=(u == 0 and z == 0 and at == 0),
                             stop=False,
                         )
 
         def multiply_a(c, b):
-            for u in range(PAIR):
-                q = b * PAIR + u
-                nc.tensor.matmul_mx(
-                    out=sums[c][b][:, u, :],
-                    lhsT=qa_codes[:, P * q : P * (q + 1)].bitcast(FP8X4),
-                    lhsT_scale=qa_plane[:, 0, P * q : P * (q + 1)],
-                    rhs=ka_codes[c][:].bitcast(FP8X4),
-                    rhs_scale=ka_plane[c][:],
-                    start=False,
-                    stop=(u == PAIR - 1),
-                )
+            rows = rows_of_bank(c, b)
+            for u, q in enumerate(rows):
+                for at in range(0, widths[c], STRIP):
+                    s = (CHUNKS[c][0] + at) // STRIP
+                    nc.tensor.matmul_mx(
+                        out=sums[c][b][:, u, at : at + STRIP],
+                        lhsT=qa_codes[:, P * q : P * (q + 1)].bitcast(FP8X4),
+                        lhsT_scale=qa_plane[:, 0, P * q : P * (q + 1)],
+                        rhs=ka_codes[s][:].bitcast(FP8X4),
+                        rhs_scale=ka_plane[s][:],
+                        start=False,
+                        stop=(u == len(rows) - 1 and at + STRIP == widths[c]),
+                    )
 
         def multiply(c):
-            for b in range(PAIRS):
+            for b in range(len(sums[c])):
                 multiply_b(c, b)
-            for b in range(PAIRS):
+            for b in range(len(sums[c])):
                 multiply_a(c, b)
 
-        def chunk_max_with_copy(c, b):
-            for u in range(PAIR):
-                q = b * PAIR + u
+        def chunk_max(c, b):
+            rows = rows_of_bank(c, b)
+            nc.vector.tensor_reduce(
+                out=neg_chunk_max[:, rows.start : rows.stop, c], in_=sums[c][b][:], axis=AXIS.X, op=ALU.max, negate=True
+            )
+
+        def exponentials(c, b):
+            for u, q in enumerate(rows_of_bank(c, b)):
+                nc.scalar.activation(
+                    out=exps[:, q, columns(c)], in_=sums[c][b][:, u, :], func=ACT.Exp, bias=neg_chunk_max[:, q, c : c + 1]
+                )
+
+        def add_offset(c, b):
+            rows = rows_of_bank(c, b)
+            nc.vector.tensor_tensor(
+                out=a_plus_of[:, rows.start : rows.stop, columns(c)],
+                in0=sums[c][b][:],
+                in1=of_row[:, columns(c)].unsqueeze(1).to_broadcast([P, len(rows), widths[c]]),
+                op=ALU.add,
+            )
+
+        def through_copy(c, b):
+            neg_a = sb.tile([P, BANK // widths[c], widths[c]], F32, name="neg_a%d" % c)
+            for u, q in enumerate(rows_of_bank(c, b)):
                 nc.vector.tensor_scalar(
                     out=neg_a[:, u, :],
                     in0=sums[c][b][:, u, :],
@@ -179,76 +216,60 @@ def tile_mix_behind_the_best_column_kernel(
                     out=exps[:, q, columns(c)], in_=neg_a[:, u, :], func=ACT.Exp, scale=-1.0, bias=neg_chunk_max[:, q, c : c + 1]
                 )
 
-        def chunk_max(c, b):
-            nc.vector.tensor_reduce(
-                out=neg_chunk_max[:, b * PAIR : (b + 1) * PAIR, c], in_=sums[c][b][:], axis=AXIS.X, op=ALU.max, negate=True
-            )
-
-        def exponentials(c, b):
-            for u in range(PAIR):
-                q = b * PAIR + u
-                nc.scalar.activation(
-                    out=exps[:, q, columns(c)], in_=sums[c][b][:, u, :], func=ACT.Exp, bias=neg_chunk_max[:, q, c : c + 1]
-                )
-
-        def add_offset(c, b):
-            nc.vector.tensor_tensor(
-                out=a_plus_of[:, b * PAIR : (b + 1) * PAIR, columns(c)],
-                in0=sums[c][b][:],
-                in1=of_row[:, columns(c)].unsqueeze(1).to_broadcast([P, PAIR, CHUNK]),
-                op=ALU.add,
-            )
-
-        round_and_interleave(0, VECTOR_SHARE_FIRST)
-        quantise(0)
+        for s in (0, 1):
+            round_on_scalar(0, s, VECTOR_SHARE)
+            round_on_vector(0, s, VECTOR_SHARE)
+        for s in (0, 1):
+            quantise(s)
         multiply(0)
-        last = CHUNKS - 1
-        for c in range(1, last):
-            round_and_interleave(c, VECTOR_SHARE)
-            if c > 1:
-                exponentials(c - 2, 1)
-            chunk_max(c - 1, 0)
-            exponentials(c - 1, 0)
-            quantise(c)
-            chunk_max(c - 1, 1)
-            if c == 1:
+        for c in (1, 2):
+            s = c + 1
+            round_on_scalar(c, s, GPSIMD_SHARE)
+            round_on_gpsimd(c, s, GPSIMD_SHARE)
+            for q in (2 * c - 2, 2 * c - 1):
+                chunk_max(0, q)
+                exponentials(0, q)
+            if c == 2:
                 add_offset(0, 0)
-            multiply(c)
-        round_and_interleave(last, VECTOR_SHARE_FIRST)
-        exponentials(last - 2, 1)
-        quantise(last)
-        chunk_max(last - 1, 0)
-        exponentials(last - 1, 0)
-        chunk_max_with_copy(last - 1, 1)
-        for b in range(PAIRS):
-            multiply_b(last, b)
-            multiply_a(last, b)
-            chunk_max(last, b)
-            exponentials(last, b)
-        add_offset(1, 0)
+            quantise(s)
+            if c == 1:
+                multiply(c)
+        for c in (1, 2):
+            for b in range(2):
+                if c == 2:
+                    multiply_b(c, b)
+                    multiply_a(c, b)
+            chunk_max(c, 0)
+            exponentials(c, 0)
+            through_copy(c, 1)
         nc.vector.tensor_reduce(out=neg_row_max[:], in_=neg_chunk_max[:], axis=AXIS.X, op=ALU.min)
         for q in range(ROW_TILES):
             nc.scalar.activation(
                 out=rescale[:, q, :], in_=neg_chunk_max[:, q, :], func=ACT.Exp, scale=-1.0, bias=neg_row_max[:, q : q + 1]
             )
-        for c in range(2, CHUNKS):
-            add_offset(c, 0)
-        for c in (0, 1, last):
-            add_offset(c, 1)
+        add_offset(0, 1)
+        add_offset(1, 0)
+        add_offset(2, 0)
+        add_offset(0, 2)
+        add_offset(0, 3)
 
         for q in range(ROW_TILES):
-            pieces = ((0, 1), (2, 3))
-            for piece in pieces:
-                cols = slice(piece[0] * CHUNK, (piece[-1] + 1) * CHUNK)
-                logs = sb.tile([P, len(piece), CHUNK], F32, name="logs%d_%d" % (q, piece[0]))
-                for n, c in enumerate(piece):
-                    nc.scalar.activation(
-                        out=logs[:, n, :], in_=exps[:, q, columns(c)], func=ACT.Ln, bias=1.0, scale=rescale[:, q, c : c + 1]
-                    )
-                result = sb.tile([P, len(piece) * CHUNK], F32, name="result%d_%d" % (q, piece[0]))
+            for half in range(2):
+                cols = slice(half * BANK, (half + 1) * BANK)
+                logs = sb.tile([P, BANK], F32, name="logs%d_%d" % (q, half))
+                for c, (lo, hi) in enumerate(CHUNKS):
+                    if lo // BANK == half:
+                        nc.scalar.activation(
+                            out=logs[:, lo - cols.start : hi - cols.start],
+                            in_=exps[:, q, lo:hi],
+                            func=ACT.Ln,
+                            bias=1.0,
+                            scale=rescale[:, q, c : c + 1],
+                        )
+                result = sb.tile([P, BANK], F32, name="result%d_%d" % (q, half))
                 nc.vector.scalar_tensor_tensor(
                     out=result[:],
-                    in0=logs[:].rearrange("p n w -> p (n w)"),
+                    in0=logs[:],
                     scalar=neg_row_max[:, q : q + 1],
                     in1=a_plus_of[:, q, cols],
                     op0=ALU.subtract,

@@ -19,11 +19,17 @@ AXIS = mybir.AxisListType
 
 P = 128
 PACK = 4
+QUADRANT = 32
+SCALE_ROWS = 4
 ROW_TILES = Q // P
 L_PASSES = L // (P * PACK)
 BANK = 512
+BANKS = ROW_TILES * I // BANK
 STRIP = 256
+RUN = 4
+
 CHUNKS = ((0, 512), (512, 768), (768, 1024))
+WIDE, MIDDLE, LAST = range(len(CHUNKS))
 VECTOR_SHARE = 160
 GPSIMD_SHARE = 128
 
@@ -52,6 +58,7 @@ def tile_mix_behind_the_best_column_kernel(
         of_column = sb.tile([P, I // P], F32, name="of_column")
         of_row = sb.tile([P, I], F32, name="of_row")
         identity = sb.tile([P, P], F32, name="identity")
+        neg_a = [sb.tile([P, BANK // w, w], F32, name="neg_a%d" % c) for c, w in enumerate(widths)]
         neg_chunk_max = sb.tile([P, ROW_TILES, len(CHUNKS)], F32, name="neg_chunk_max")
         neg_row_max = sb.tile([P, ROW_TILES], F32, name="neg_row_max")
         rescale = sb.tile([P, ROW_TILES, len(CHUNKS)], F32, name="rescale")
@@ -61,7 +68,13 @@ def tile_mix_behind_the_best_column_kernel(
         def columns(c):
             return slice(CHUNKS[c][0], CHUNKS[c][1])
 
-        def rows_of_bank(c, b):
+        def strips_of(c):
+            return range(CHUNKS[c][0] // STRIP, CHUNKS[c][1] // STRIP)
+
+        def banks_of(c):
+            return range(ROW_TILES * widths[c] // BANK)
+
+        def row_tiles_in(c, b):
             count = BANK // widths[c]
             return range(b * count, (b + 1) * count)
 
@@ -70,9 +83,9 @@ def tile_mix_behind_the_best_column_kernel(
         make_identity(nc, identity[:])
 
         def load_scale_rows(plane, scales, rows):
-            by_row = scales.rearrange("z (g r) n -> r g z n", r=4)
+            by_row = scales.rearrange("z (g r) n -> r g z n", r=SCALE_ROWS)
             for r in rows:
-                nc.sync.dma_start(out=plane[r:P:32].bitcast(I32), in_=by_row[r].bitcast(I32))
+                nc.sync.dma_start(out=plane[r:P:QUADRANT].bitcast(I32), in_=by_row[r].bitcast(I32))
 
         def load_ka(c):
             nc.sync.dma_start(out=ka_raw[c][:], in_=ka.rearrange("(p t) n -> p t n", t=PACK)[:, :, columns(c)])
@@ -83,35 +96,36 @@ def tile_mix_behind_the_best_column_kernel(
 
         nc.sync.dma_start(out=of_column[:], in_=of[0].rearrange("(p j) -> p j", p=P))
         nc.sync.dma_start(out=qb_codes[:].bitcast(I32), in_=qb_words.rearrange("z p b -> p z b").bitcast(I32))
-        load_scale_rows(qb_plane, qb_scales, range(4))
-        load_scale_rows(kb_plane, kb_scales, range(2))
-        load_kb(0)
-        load_scale_rows(kb_plane, kb_scales, range(2, 4))
-        load_ka(0)
+        load_scale_rows(qb_plane, qb_scales, range(SCALE_ROWS))
+        load_scale_rows(kb_plane, kb_scales, range(SCALE_ROWS // 2))
+        load_kb(WIDE)
+        load_scale_rows(kb_plane, kb_scales, range(SCALE_ROWS // 2, SCALE_ROWS))
+        load_ka(WIDE)
         nc.sync.dma_start(out=qa_codes[:].bitcast(I32), in_=qa_words[0].rearrange("p n t -> p (n t)").bitcast(I32))
-        load_scale_rows(qa_plane, qa_scales, range(4))
-        for c in range(1, len(CHUNKS)):
+        load_scale_rows(qa_plane, qa_scales, range(SCALE_ROWS))
+        for c in (MIDDLE, LAST):
             load_ka(c)
             load_kb(c)
 
-        bank_tags = ["bank%d" % n for n in range(8)]
-        for half in range(2):
-            spread = psum.tile([P, PACK, P], F32, name="spread%d" % half, tag=bank_tags[half - 2])
-            for j in range(PACK):
-                source = of_column[:, PACK * half + j : PACK * half + j + 1].to_broadcast([P, P])
+        bank_tags = ["bank%d" % n for n in range(BANKS)]
+        per_bank = BANK // P
+        for half, tag in enumerate(bank_tags[-2:]):
+            spread = psum.tile([P, per_bank, P], F32, name="spread%d" % half, tag=tag)
+            for j in range(per_bank):
+                source = of_column[:, per_bank * half + j : per_bank * half + j + 1].to_broadcast([P, P])
                 nc.tensor.transpose(spread[:, j, :], source, identity[:])
             nc.scalar.copy(
-                out=of_row[:].rearrange("p (n j) -> p n j", n=P)[:, :, PACK * half : PACK * (half + 1)],
+                out=of_row[:].rearrange("p (n j) -> p n j", n=P)[:, :, per_bank * half : per_bank * (half + 1)],
                 in_=spread[:].rearrange("p j n -> p n j"),
             )
 
         sums = []
         for c, w in enumerate(widths):
-            first = ROW_TILES * CHUNKS[c][0] // BANK
+            first_bank = ROW_TILES * CHUNKS[c][0] // BANK
             sums.append(
                 [
-                    psum.tile([P, BANK // w, w], F32, name="sums%d_%d" % (c, b), tag=bank_tags[first + b])
-                    for b in range(ROW_TILES * w // BANK)
+                    psum.tile([P, BANK // w, w], F32, name="sums%d_%d" % (c, b), tag=bank_tags[first_bank + b])
+                    for b in banks_of(c)
                 ]
             )
 
@@ -121,11 +135,15 @@ def tile_mix_behind_the_best_column_kernel(
 
         def round_on_scalar(c, s, lo):
             target, source = strip_views(c, s, lo, STRIP)
-            nc.scalar.copy(out=target.rearrange("p (n i) t -> p n t i", i=4), in_=source.rearrange("p t (n i) -> p n t i", i=4))
+            nc.scalar.copy(
+                out=target.rearrange("p (n i) t -> p n t i", i=RUN), in_=source.rearrange("p t (n i) -> p n t i", i=RUN)
+            )
 
         def round_on_vector(c, s, hi):
             target, source = strip_views(c, s, 0, hi)
-            nc.vector.tensor_copy(out=target.rearrange("p (n i) t -> p n t i", i=4), in_=source.rearrange("p t (n i) -> p n t i", i=4))
+            nc.vector.tensor_copy(
+                out=target.rearrange("p (n i) t -> p n t i", i=RUN), in_=source.rearrange("p t (n i) -> p n t i", i=RUN)
+            )
 
         def round_on_gpsimd(c, s, hi):
             target, source = strip_views(c, s, 0, hi)
@@ -141,8 +159,8 @@ def tile_mix_behind_the_best_column_kernel(
             )
 
         def multiply_b(c, b):
-            step = BANK if widths[c] == BANK else P
-            for u, q in enumerate(rows_of_bank(c, b)):
+            step = BANK if c == WIDE else P
+            for u, q in enumerate(row_tiles_in(c, b)):
                 for z in range(L_PASSES):
                     for at in range(0, widths[c], step):
                         nc.tensor.matmul_mx(
@@ -156,10 +174,10 @@ def tile_mix_behind_the_best_column_kernel(
                         )
 
         def multiply_a(c, b):
-            rows = rows_of_bank(c, b)
+            rows = row_tiles_in(c, b)
             for u, q in enumerate(rows):
-                for at in range(0, widths[c], STRIP):
-                    s = (CHUNKS[c][0] + at) // STRIP
+                for s in strips_of(c):
+                    at = s * STRIP - CHUNKS[c][0]
                     nc.tensor.matmul_mx(
                         out=sums[c][b][:, u, at : at + STRIP],
                         lhsT=qa_codes[:, P * q : P * (q + 1)].bitcast(FP8X4),
@@ -167,29 +185,46 @@ def tile_mix_behind_the_best_column_kernel(
                         rhs=ka_codes[s][:].bitcast(FP8X4),
                         rhs_scale=ka_plane[s][:],
                         start=False,
-                        stop=(u == len(rows) - 1 and at + STRIP == widths[c]),
+                        stop=(q == rows[-1] and s == strips_of(c)[-1]),
                     )
 
         def multiply(c):
-            for b in range(len(sums[c])):
+            for b in banks_of(c):
                 multiply_b(c, b)
-            for b in range(len(sums[c])):
+            for b in banks_of(c):
                 multiply_a(c, b)
 
-        def chunk_max(c, b):
-            rows = rows_of_bank(c, b)
-            nc.vector.tensor_reduce(
-                out=neg_chunk_max[:, rows.start : rows.stop, c], in_=sums[c][b][:], axis=AXIS.X, op=ALU.max, negate=True
-            )
-
-        def exponentials(c, b):
-            for u, q in enumerate(rows_of_bank(c, b)):
-                nc.scalar.activation(
-                    out=exps[:, q, columns(c)], in_=sums[c][b][:, u, :], func=ACT.Exp, bias=neg_chunk_max[:, q, c : c + 1]
+        def max_and_exp(c, b):
+            rows = row_tiles_in(c, b)
+            if b == banks_of(c)[-1]:
+                for u, q in enumerate(rows):
+                    nc.vector.tensor_scalar(
+                        out=neg_a[c][:, u, :],
+                        in0=sums[c][b][:, u, :],
+                        scalar1=-1.0,
+                        scalar2=None,
+                        op0=ALU.mult,
+                        op1=ALU.min,
+                        accum_out=neg_chunk_max[:, q, c : c + 1],
+                    )
+                    nc.scalar.activation(
+                        out=exps[:, q, columns(c)],
+                        in_=neg_a[c][:, u, :],
+                        func=ACT.Exp,
+                        scale=-1.0,
+                        bias=neg_chunk_max[:, q, c : c + 1],
+                    )
+            else:
+                nc.vector.tensor_reduce(
+                    out=neg_chunk_max[:, rows.start : rows.stop, c], in_=sums[c][b][:], axis=AXIS.X, op=ALU.max, negate=True
                 )
+                for u, q in enumerate(rows):
+                    nc.scalar.activation(
+                        out=exps[:, q, columns(c)], in_=sums[c][b][:, u, :], func=ACT.Exp, bias=neg_chunk_max[:, q, c : c + 1]
+                    )
 
-        def add_offset(c, b):
-            rows = rows_of_bank(c, b)
+        def add_offset_on_vector(c, b):
+            rows = row_tiles_in(c, b)
             nc.vector.tensor_tensor(
                 out=a_plus_of[:, rows.start : rows.stop, columns(c)],
                 in0=sums[c][b][:],
@@ -197,82 +232,68 @@ def tile_mix_behind_the_best_column_kernel(
                 op=ALU.add,
             )
 
-        def through_copy(c, b):
-            neg_a = sb.tile([P, BANK // widths[c], widths[c]], F32, name="neg_a%d" % c)
-            for u, q in enumerate(rows_of_bank(c, b)):
-                nc.vector.tensor_scalar(
-                    out=neg_a[:, u, :],
-                    in0=sums[c][b][:, u, :],
-                    scalar1=-1.0,
-                    scalar2=None,
-                    op0=ALU.mult,
-                    op1=ALU.min,
-                    accum_out=neg_chunk_max[:, q, c : c + 1],
-                )
+        def add_offset_on_gpsimd(c):
+            for u, q in enumerate(row_tiles_in(c, banks_of(c)[-1])):
                 nc.gpsimd.tensor_tensor(
-                    out=a_plus_of[:, q, columns(c)], in0=of_row[:, columns(c)], in1=neg_a[:, u, :], op=ALU.subtract
-                )
-                nc.scalar.activation(
-                    out=exps[:, q, columns(c)], in_=neg_a[:, u, :], func=ACT.Exp, scale=-1.0, bias=neg_chunk_max[:, q, c : c + 1]
+                    out=a_plus_of[:, q, columns(c)], in0=of_row[:, columns(c)], in1=neg_a[c][:, u, :], op=ALU.subtract
                 )
 
-        for s in (0, 1):
-            round_on_scalar(0, s, VECTOR_SHARE)
-            round_on_vector(0, s, VECTOR_SHARE)
-        for s in (0, 1):
+        for s in strips_of(WIDE):
+            round_on_scalar(WIDE, s, VECTOR_SHARE)
+            round_on_vector(WIDE, s, VECTOR_SHARE)
+        for s in strips_of(WIDE):
             quantise(s)
-        multiply(0)
-        for c in (1, 2):
-            s = c + 1
+        multiply(WIDE)
+
+        half_of_wide = len(banks_of(WIDE)) // 2
+        for n, c in enumerate((MIDDLE, LAST)):
+            s = strips_of(c)[0]
             round_on_scalar(c, s, GPSIMD_SHARE)
             round_on_gpsimd(c, s, GPSIMD_SHARE)
-            for q in (2 * c - 2, 2 * c - 1):
-                chunk_max(0, q)
-                exponentials(0, q)
-            if c == 2:
-                add_offset(0, 0)
+            for b in range(n * half_of_wide, (n + 1) * half_of_wide):
+                max_and_exp(WIDE, b)
             quantise(s)
-            if c == 1:
-                multiply(c)
-        for c in (1, 2):
-            for b in range(2):
-                if c == 2:
-                    multiply_b(c, b)
-                    multiply_a(c, b)
-            chunk_max(c, 0)
-            exponentials(c, 0)
-            through_copy(c, 1)
+        multiply(MIDDLE)
+        for b in banks_of(LAST):
+            multiply_b(LAST, b)
+            multiply_a(LAST, b)
+        for c in (MIDDLE, LAST):
+            for b in banks_of(c):
+                max_and_exp(c, b)
+
+        for c in (MIDDLE, WIDE, LAST):
+            add_offset_on_gpsimd(c)
+
         nc.vector.tensor_reduce(out=neg_row_max[:], in_=neg_chunk_max[:], axis=AXIS.X, op=ALU.min)
         for q in range(ROW_TILES):
             nc.scalar.activation(
                 out=rescale[:, q, :], in_=neg_chunk_max[:, q, :], func=ACT.Exp, scale=-1.0, bias=neg_row_max[:, q : q + 1]
             )
-        add_offset(0, 1)
-        add_offset(1, 0)
-        add_offset(2, 0)
-        add_offset(0, 2)
-        add_offset(0, 3)
+        for q in range(ROW_TILES):
+            for c in range(len(CHUNKS)):
+                for b in banks_of(c)[:-1]:
+                    if row_tiles_in(c, b)[0] == q:
+                        add_offset_on_vector(c, b)
 
         for q in range(ROW_TILES):
-            for half in range(2):
-                cols = slice(half * BANK, (half + 1) * BANK)
-                logs = sb.tile([P, BANK], F32, name="logs%d_%d" % (q, half))
+            for first in range(0, I, BANK):
+                logs = sb.tile([P, BANK], F32, name="logs%d_%d" % (q, first))
                 for c, (lo, hi) in enumerate(CHUNKS):
-                    if lo // BANK == half:
+                    if first <= lo < first + BANK:
                         nc.scalar.activation(
-                            out=logs[:, lo - cols.start : hi - cols.start],
+                            out=logs[:, lo - first : hi - first],
                             in_=exps[:, q, lo:hi],
                             func=ACT.Ln,
                             bias=1.0,
                             scale=rescale[:, q, c : c + 1],
                         )
-                result = sb.tile([P, BANK], F32, name="result%d_%d" % (q, half))
+                result = sb.tile([P, BANK], F32, name="result%d_%d" % (q, first))
                 nc.vector.scalar_tensor_tensor(
                     out=result[:],
                     in0=logs[:],
                     scalar=neg_row_max[:, q : q + 1],
-                    in1=a_plus_of[:, q, cols],
+                    in1=a_plus_of[:, q, first : first + BANK],
                     op0=ALU.subtract,
                     op1=ALU.subtract,
                 )
-                nc.sync.dma_start(out=out[P * q : P * (q + 1), cols], in_=result[:])
+                nc.sync.dma_start(out=out[P * q : P * (q + 1), first : first + BANK], in_=result[:])

from contextlib import ExitStack

import concourse.mybir as mybir
from concourse.masks import make_identity

K, L, Q, I = 512, 1024, 512, 1024
FLOPS = 2 * Q * I * (K + L)

F32 = mybir.dt.float32
BF16 = mybir.dt.bfloat16
I32 = mybir.dt.int32
U32 = mybir.dt.uint32
U8 = mybir.dt.uint8
FP8X4 = mybir.dt.float8_e4m3fn_x4
FP4X4 = mybir.dt.float4_e2m1fn_x4
ACT = mybir.ActivationFunctionType
ALU = mybir.AluOpType
AXIS = mybir.AxisListType

P = 128
PACK = 4
QUADRANT = 32
SCALE_ROWS = 4
ROW_TILES = Q // P
L_PASSES = L // (P * PACK)
BANK = 512
BANKS = ROW_TILES * I // BANK
STRIP = 256
RUN = 4

CHUNKS = ((0, 512), (512, 768), (768, 1024))
WIDE, MIDDLE, LAST = range(len(CHUNKS))
VECTOR_SHARE = 160
GPSIMD_SHARE = 128


def tile_mix_behind_the_best_column_kernel(
    tc, qa_words, qa_scales, ka, qb_words, qb_scales, kb_words, kb_scales, of, out
):
    nc = tc.nc
    with ExitStack() as ctx:
        sb = ctx.enter_context(tc.tile_pool(name="sb", bufs=1))
        psum = ctx.enter_context(tc.psum_pool(name="psum", bufs=1))
        ctx.enter_context(tc.manual_schedule())

        widths = [hi - lo for lo, hi in CHUNKS]
        strips = range(I // STRIP)
        qa_codes = sb.tile([P, Q], U32, name="qa_codes", align_bytes=64)
        qa_plane = sb.tile([P, 1, Q], U8, name="qa_plane", align_bytes=64)
        qb_codes = sb.tile([P, L_PASSES, 2 * Q], U8, name="qb_codes", align_bytes=64)
        qb_plane = sb.tile([P, L_PASSES, Q], U8, name="qb_plane", align_bytes=64)
        kb_plane = sb.tile([P, L_PASSES, I], U8, name="kb_plane", align_bytes=64)
        kb_codes = [sb.tile([P, L_PASSES, w], U32, name="kb_codes%d" % c, align_bytes=64) for c, w in enumerate(widths)]
        ka_raw = [sb.tile([P, PACK, w], F32, name="ka_raw%d" % c) for c, w in enumerate(widths)]
        ka_bf16 = [sb.tile([P, STRIP, PACK], BF16, name="ka_bf16_%d" % s, align_bytes=64) for s in strips]
        ka_codes = [sb.tile([P, STRIP], U32, name="ka_codes%d" % s, align_bytes=64) for s in strips]
        ka_plane = [sb.tile([P, STRIP], U8, name="ka_plane%d" % s, align_bytes=64) for s in strips]
        of_column = sb.tile([P, I // P], F32, name="of_column")
        of_row = sb.tile([P, I], F32, name="of_row")
        identity = sb.tile([P, P], F32, name="identity")
        neg_a = [sb.tile([P, BANK // w, w], F32, name="neg_a%d" % c) for c, w in enumerate(widths)]
        neg_chunk_max = sb.tile([P, ROW_TILES, len(CHUNKS)], F32, name="neg_chunk_max")
        neg_row_max = sb.tile([P, ROW_TILES], F32, name="neg_row_max")
        rescale = sb.tile([P, ROW_TILES, len(CHUNKS)], F32, name="rescale")
        exps = sb.tile([P, ROW_TILES, I], F32, name="exps")
        a_plus_of = sb.tile([P, ROW_TILES, I], F32, name="a_plus_of")

        def columns(c):
            return slice(CHUNKS[c][0], CHUNKS[c][1])

        def strips_of(c):
            return range(CHUNKS[c][0] // STRIP, CHUNKS[c][1] // STRIP)

        def banks_of(c):
            return range(ROW_TILES * widths[c] // BANK)

        def row_tiles_in(c, b):
            count = BANK // widths[c]
            return range(b * count, (b + 1) * count)

        for plane in (qb_plane, kb_plane, qa_plane):
            nc.vector.memset(plane[:].rearrange("p z n -> p (z n)").bitcast(I32), 0)
        make_identity(nc, identity[:])

        def load_scale_rows(plane, scales, rows):
            by_row = scales.rearrange("z (g r) n -> r g z n", r=SCALE_ROWS)
            for r in rows:
                nc.sync.dma_start(out=plane[r:P:QUADRANT].bitcast(I32), in_=by_row[r].bitcast(I32))

        def load_ka(c):
            nc.sync.dma_start(out=ka_raw[c][:], in_=ka.rearrange("(p t) n -> p t n", t=PACK)[:, :, columns(c)])

        def load_kb(c):
            words = kb_words.rearrange("z p n t -> p z (n t)").bitcast(I32)
            nc.sync.dma_start(out=kb_codes[c][:].bitcast(I32), in_=words[:, :, columns(c)])

        nc.sync.dma_start(out=of_column[:], in_=of[0].rearrange("(p j) -> p j", p=P))
        nc.sync.dma_start(out=qb_codes[:].bitcast(I32), in_=qb_words.rearrange("z p b -> p z b").bitcast(I32))
        load_scale_rows(qb_plane, qb_scales, range(SCALE_ROWS))
        load_scale_rows(kb_plane, kb_scales, range(SCALE_ROWS // 2))
        load_kb(WIDE)
        load_scale_rows(kb_plane, kb_scales, range(SCALE_ROWS // 2, SCALE_ROWS))
        load_ka(WIDE)
        nc.sync.dma_start(out=qa_codes[:].bitcast(I32), in_=qa_words[0].rearrange("p n t -> p (n t)").bitcast(I32))
        load_scale_rows(qa_plane, qa_scales, range(SCALE_ROWS))
        for c in (MIDDLE, LAST):
            load_ka(c)
            load_kb(c)

        bank_tags = ["bank%d" % n for n in range(BANKS)]
        per_bank = BANK // P
        for half, tag in enumerate(bank_tags[-2:]):
            spread = psum.tile([P, per_bank, P], F32, name="spread%d" % half, tag=tag)
            for j in range(per_bank):
                source = of_column[:, per_bank * half + j : per_bank * half + j + 1].to_broadcast([P, P])
                nc.tensor.transpose(spread[:, j, :], source, identity[:])
            nc.scalar.copy(
                out=of_row[:].rearrange("p (n j) -> p n j", n=P)[:, :, per_bank * half : per_bank * (half + 1)],
                in_=spread[:].rearrange("p j n -> p n j"),
            )

        sums = []
        for c, w in enumerate(widths):
            first_bank = ROW_TILES * CHUNKS[c][0] // BANK
            sums.append(
                [
                    psum.tile([P, BANK // w, w], F32, name="sums%d_%d" % (c, b), tag=bank_tags[first_bank + b])
                    for b in banks_of(c)
                ]
            )

        def strip_views(c, s, lo, hi):
            at = s * STRIP - CHUNKS[c][0]
            return ka_bf16[s][:, lo:hi, :], ka_raw[c][:, :, at + lo : at + hi]

        def round_on_scalar(c, s, lo):
            target, source = strip_views(c, s, lo, STRIP)
            nc.scalar.copy(
                out=target.rearrange("p (n i) t -> p n t i", i=RUN), in_=source.rearrange("p t (n i) -> p n t i", i=RUN)
            )

        def round_on_vector(c, s, hi):
            target, source = strip_views(c, s, 0, hi)
            nc.vector.tensor_copy(
                out=target.rearrange("p (n i) t -> p n t i", i=RUN), in_=source.rearrange("p t (n i) -> p n t i", i=RUN)
            )

        def round_on_gpsimd(c, s, hi):
            target, source = strip_views(c, s, 0, hi)
            nc.gpsimd.tensor_scalar(
                out=target, in0=source.rearrange("p t n -> p n t"), scalar1=1.0, scalar2=0.0, op0=ALU.mult, op1=ALU.add
            )

        def quantise(s):
            nc.vector.quantize_mx(
                out=ka_codes[s][:].bitcast(FP8X4),
                scales=ka_plane[s][:],
                in_=ka_bf16[s][:].rearrange("p n t -> p (n t)"),
            )

        def multiply_b(c, b):
            step = BANK if c == WIDE else P
            for u, q in enumerate(row_tiles_in(c, b)):
                for z in range(L_PASSES):
                    for at in range(0, widths[c], step):
                        nc.tensor.matmul_mx(
                            out=sums[c][b][:, u, at : at + step],
                            lhsT=qb_codes[:, z, 2 * P * q : 2 * P * (q + 1)].bitcast(FP4X4),
                            lhsT_scale=qb_plane[:, z, P * q : P * (q + 1)],
                            rhs=kb_codes[c][:, z, at : at + step].bitcast(FP8X4),
                            rhs_scale=kb_plane[:, z, CHUNKS[c][0] + at : CHUNKS[c][0] + at + step],
                            start=(u == 0 and z == 0 and at == 0),
                            stop=False,
                        )

        def multiply_a(c, b):
            rows = row_tiles_in(c, b)
            for u, q in enumerate(rows):
                for s in strips_of(c):
                    at = s * STRIP - CHUNKS[c][0]
                    nc.tensor.matmul_mx(
                        out=sums[c][b][:, u, at : at + STRIP],
                        lhsT=qa_codes[:, P * q : P * (q + 1)].bitcast(FP8X4),
                        lhsT_scale=qa_plane[:, 0, P * q : P * (q + 1)],
                        rhs=ka_codes[s][:].bitcast(FP8X4),
                        rhs_scale=ka_plane[s][:],
                        start=False,
                        stop=(q == rows[-1] and s == strips_of(c)[-1]),
                    )

        def multiply(c):
            for b in banks_of(c):
                multiply_b(c, b)
            for b in banks_of(c):
                multiply_a(c, b)

        def max_and_exp(c, b):
            rows = row_tiles_in(c, b)
            if b == banks_of(c)[-1]:
                for u, q in enumerate(rows):
                    nc.vector.tensor_scalar(
                        out=neg_a[c][:, u, :],
                        in0=sums[c][b][:, u, :],
                        scalar1=-1.0,
                        scalar2=None,
                        op0=ALU.mult,
                        op1=ALU.min,
                        accum_out=neg_chunk_max[:, q, c : c + 1],
                    )
                    nc.scalar.activation(
                        out=exps[:, q, columns(c)],
                        in_=neg_a[c][:, u, :],
                        func=ACT.Exp,
                        scale=-1.0,
                        bias=neg_chunk_max[:, q, c : c + 1],
                    )
            else:
                nc.vector.tensor_reduce(
                    out=neg_chunk_max[:, rows.start : rows.stop, c], in_=sums[c][b][:], axis=AXIS.X, op=ALU.max, negate=True
                )
                for u, q in enumerate(rows):
                    nc.scalar.activation(
                        out=exps[:, q, columns(c)], in_=sums[c][b][:, u, :], func=ACT.Exp, bias=neg_chunk_max[:, q, c : c + 1]
                    )

        def add_offset_on_vector(c, b):
            rows = row_tiles_in(c, b)
            nc.vector.tensor_tensor(
                out=a_plus_of[:, rows.start : rows.stop, columns(c)],
                in0=sums[c][b][:],
                in1=of_row[:, columns(c)].unsqueeze(1).to_broadcast([P, len(rows), widths[c]]),
                op=ALU.add,
            )

        def add_offset_on_gpsimd(c):
            for u, q in enumerate(row_tiles_in(c, banks_of(c)[-1])):
                nc.gpsimd.tensor_tensor(
                    out=a_plus_of[:, q, columns(c)], in0=of_row[:, columns(c)], in1=neg_a[c][:, u, :], op=ALU.subtract
                )

        for s in strips_of(WIDE):
            round_on_scalar(WIDE, s, VECTOR_SHARE)
            round_on_vector(WIDE, s, VECTOR_SHARE)
        for s in strips_of(WIDE):
            quantise(s)
        multiply(WIDE)

        half_of_wide = len(banks_of(WIDE)) // 2
        for n, c in enumerate((MIDDLE, LAST)):
            s = strips_of(c)[0]
            round_on_scalar(c, s, GPSIMD_SHARE)
            round_on_gpsimd(c, s, GPSIMD_SHARE)
            for b in range(n * half_of_wide, (n + 1) * half_of_wide):
                max_and_exp(WIDE, b)
            quantise(s)
        multiply(MIDDLE)
        for b in banks_of(LAST):
            multiply_b(LAST, b)
            multiply_a(LAST, b)
        for c in (MIDDLE, LAST):
            for b in banks_of(c):
                max_and_exp(c, b)

        for c in (MIDDLE, WIDE, LAST):
            add_offset_on_gpsimd(c)

        nc.vector.tensor_reduce(out=neg_row_max[:], in_=neg_chunk_max[:], axis=AXIS.X, op=ALU.min)
        for q in range(ROW_TILES):
            nc.scalar.activation(
                out=rescale[:, q, :], in_=neg_chunk_max[:, q, :], func=ACT.Exp, scale=-1.0, bias=neg_row_max[:, q : q + 1]
            )
        for q in range(ROW_TILES):
            for c in range(len(CHUNKS)):
                for b in banks_of(c)[:-1]:
                    if row_tiles_in(c, b)[0] == q:
                        add_offset_on_vector(c, b)

        for q in range(ROW_TILES):
            for first in range(0, I, BANK):
                logs = sb.tile([P, BANK], F32, name="logs%d_%d" % (q, first))
                for c, (lo, hi) in enumerate(CHUNKS):
                    if first <= lo < first + BANK:
                        nc.scalar.activation(
                            out=logs[:, lo - first : hi - first],
                            in_=exps[:, q, lo:hi],
                            func=ACT.Ln,
                            bias=1.0,
                            scale=rescale[:, q, c : c + 1],
                        )
                result = sb.tile([P, BANK], F32, name="result%d_%d" % (q, first))
                nc.vector.scalar_tensor_tensor(
                    out=result[:],
                    in0=logs[:],
                    scalar=neg_row_max[:, q : q + 1],
                    in1=a_plus_of[:, q, first : first + BANK],
                    op0=ALU.subtract,
                    op1=ALU.subtract,
                )
                nc.sync.dma_start(out=out[P * q : P * (q + 1), first : first + BANK], in_=result[:])
